import numpy as np, ml_dtypes
CORES = [23,39,55,63,87,103,111,127,18,34,50,58,82,98,106,122]
N = 16
T, G, CAP = 8192, 8192, 2048
def entries(a): return a.T.reshape(-1)
def pack(v, P): return np.ascontiguousarray(np.asarray(v, np.int32).reshape(-1, P).T)
def lists(rng, how):
    S = rng.integers(0, T, (N, 2 * CAP)); P = np.stack([rng.permutation(G)[:2 * CAP] for r in range(N)])
    if how == "alike": S[:] = rng.integers(0, T, (N, 1))
    if how == "edge":
        S = np.where(rng.random((N, 2 * CAP)) < 0.5, 0, T - 1); S[:, [0, CAP]] = 0; S[:, [1, CAP + 1]] = T - 1
        P[:, 1:-1] = np.stack([1 + rng.permutation(G - 2)[:2 * CAP - 2] for r in range(N)]); P[0::2, 0], P[0::2, -1] = 0, G - 1; P[1::2, 0], P[1::2, -1] = G - 1, 0
    if how == "mixed": P = np.stack([rng.permutation(2 * CAP) for r in range(N)]); P[1::2] += G - 2 * CAP
    if how == "sorted":
        S2, P2 = [-np.sort(-A.reshape(N, 2, CAP), axis=2).reshape(N, 2 * CAP) for A in (S, P)]; S, P = -np.sort(-S, axis=1), -np.sort(-P, axis=1)
        S[1::3], P[1::3] = S[1::3, ::-1].copy(), P[1::3, ::-1].copy(); S[2::3], P[2::3] = S2[2::3], P2[2::3]
    return {"snd": np.stack([pack(s, 16) for s in S]), "plc": np.stack([pack(q, 16) for q in P])}
def setup_inputs(rng):
    return dict({"x": rng.standard_normal((N, 128, T), dtype=np.float32).astype(ml_dtypes.bfloat16), "gh": rng.standard_normal((N, 128, G), dtype=np.float32).astype(ml_dtypes.bfloat16)}, **lists(rng, "uniform"))
def setup_inputs_alike(rng):
    d = setup_inputs(rng); d.update(lists(rng, "alike"))
    for k in ("x", "gh"): d[k] = (d[k].astype(np.float32) * 1048576.0).astype(d[k].dtype)
    return d
def setup_inputs_edge(rng):
    d = setup_inputs(rng); d.update(lists(rng, "edge"))
    for k in ("x", "gh"): d[k] = (d[k].astype(np.float32) * (1 / 1024.0)).astype(d[k].dtype)
    return d
def setup_inputs_mixed(rng):
    d = setup_inputs(rng); d.update(lists(rng, "mixed"))
    return d
def setup_inputs_sorted(rng):
    d = setup_inputs(rng); d.update(lists(rng, "sorted"))
    return d
def setup_inputs_zeros(rng):
    d = setup_inputs(rng); d.update(lists(rng, "zeros"))
    for r in range(N): d["x"][r][:, entries(d["snd"][r])[::2]] = 0
    return d
def check_inputs(x):
    bad = []
    if x["snd"].min() < 0 or x["snd"].max() >= T: bad.append("snd out of range")
    if x["plc"].min() < 0 or x["plc"].max() >= G: bad.append("plc out of range")
    if any(len(np.unique(a)) != a.size for a in x["plc"]): bad.append("a place is named twice")
    return bad
def reference(x, gh, snd, plc):
    y = gh.copy()
    for r in range(N):
        S = entries(snd[r]); lo, hi = (r - 1) % N, (r + 1) % N
        y[lo][:, entries(plc[lo])[CAP:]] = x[r][:, S[:CAP]]
        y[hi][:, entries(plc[hi])[:CAP]] = x[r][:, S[CAP:]]
    return {"y": y}

@@ -1,0 +1,184 @@
+from concourse.bass import DstId, RemoteDMATransfer
+from concourse.mybir import AluOpType, ActivationFunctionType
+
+N = 16
+TX, G, CAP = 8192, 8192, 2048
+WIN = G + 2 * CAP
+COPY = ActivationFunctionType.Copy
+
+SEND = [(0, 768), (768, 2048)]
+VOUT = [(0, 1024), (1024, 3072), (3072, 4096)]
+SOUT = [(4096, 5120), (5120, 7168), (7168, 8192)]
+GH = [(0, 2048), (2048, 8192)]
+ZS = 6144
+
+SCRATCH = {
+    "xs": ("sbuf", [128, TX], "bfloat16"),
+    "win": ("sbuf", [128, WIN], "bfloat16"),
+    "yt": ("sbuf", [128, G], "bfloat16"),
+    "tolo": ("sbuf", [128, CAP], "bfloat16"),
+    "tohi": ("sbuf", [128, CAP], "bfloat16"),
+    "inv": ("sbuf", [128, G], "bfloat16"),
+    "sraw": ("sbuf", [128, 256], "int32"),
+    "sfl": ("sbuf", [128, 256], "float32"),
+    "soff": ("sbuf", [128, 256], "uint16"),
+    "praw": ("sbuf", [128, 32], "int32"),
+    "poff": ("sbuf", [128, 32], "uint16"),
+    "onesf": ("sbuf", [128, 128], "float32"),
+    "onesb": ("sbuf", [128, 144], "bfloat16"),
+    "rep": ("sbuf", [128, 128], "float32"),
+    "deal": ("sbuf", [128, 144], "bfloat16"),
+    "crow": ("sbuf", [128, 512], "float32"),
+    "cown": ("sbuf", [128, 512], "float32"),
+    "tl": ("sbuf", [128, 512], "float32"),
+    "th": ("sbuf", [128, 512], "float32"),
+    "vl": ("sbuf", [128, 512], "bfloat16"),
+    "vh": ("sbuf", [128, 512], "bfloat16"),
+    "vals": ("sbuf", [128, 512], "bfloat16"),
+    "ecol": ("sbuf", [128, 16], "float32"),
+    "mx": ("sbuf", [128, 512], "float32"),
+    "yoff": ("sbuf", [128, 512], "uint16"),
+    "psE": ("psum", [128, 512], "float32"),
+    "psS": ("psum", [128, 512], "float32"),
+    "psC": ("psum", [128, 512], "float32"),
+    "psI": ("psum", [128, 512], "float32"),
+}
+SEMAPHORES = (["d_snd", "d_plc", "d_x", "d_y", "ones", "z1", "z2", "z3", "g_rep", "g_c", "g_tl", "g_th", "g_deal",
+               "v_sf", "v_po", "v_e", "v_vl", "v_so", "v_val", "v_sc", "v_mx", "v_off", "s_c", "s_vh",
+               "p_e", "p_s", "p_c", "p_i", "sent", "left", "fromlo", "fromhi"]
+              + ["d_gh%d" % i for i in range(len(GH))]
+              + ["lo%d" % i for i in range(len(SEND))] + ["hi%d" % i for i in range(len(SEND))]
+              + ["yv%d" % i for i in range(len(VOUT))] + ["ys%d" % i for i in range(len(SOUT))])
+
+
+def bits(mask):
+    return [b for b in range(mask.bit_length()) if mask >> b & 1]
+
+
+def halves(mask):
+    b = bits(mask)
+    h = len(b) // 2
+    return sum(1 << i for i in b[:h]), sum(1 << i for i in b[h:])
+
+
+def dest(topo, c):
+    rid, pid, _ = topo.addr(c)
+    return DstId(rid=rid, pnc=pid)
+
+
+def rank_program(g, core, T, topo):
+    rank = T.rank_of(core)
+    if rank is None:
+        return
+    S = T.sem
+    V, A, P, Q = g.vector, g.scalar, g.tensor, g.sync
+    lo, hi = T.cores[(rank - 1) % N], T.cores[(rank + 1) % N]
+    mlo, _ = halves(topo.mask(core, lo))
+    _, mhi = halves(topo.mask(core, hi))
+    nlo, nhi = len(bits(mlo)), len(bits(mhi))
+
+    Q.dma_start(T.sraw[0:16, :], T.snd[:, :]).then_inc(S.d_snd, 16)
+    Q.dma_start(T.xs[:, :], T.x[:, :]).then_inc(S.d_x, 16)
+    A.dma_start(T.praw[:, :], T.plc[:, :]).then_inc(S.d_plc, 16)
+
+    g.wait_ge(S.ones, 2)
+    g.affine_select(T.rep[0:16, :], T.onesf[0:16, :], [[0, 8], [1, 16]], AluOpType.is_equal, 0.0, 0, -1).then_inc(S.g_rep, 1)
+    g.iota(T.crow[0:16, :], [[16, 512]], 0, 1, allow_small_or_imprecise_dtypes=True).then_inc(S.g_c, 1)
+    g.iota(T.th[:, :], [[256, 2], [0, 32], [512, 8]], G, 0, allow_small_or_imprecise_dtypes=True).then_inc(S.g_th, 1)
+    for a in (0, 256):
+        g.iota(T.tl[:, a:a + 256], [[128, 16], [8, 2], [0, 8]], -1, 1, allow_small_or_imprecise_dtypes=True).then_inc(S.g_tl, 1)
+    g.affine_select(T.deal[:, :], T.onesb[:, :], [[0, 9], [1, 16]], AluOpType.is_equal, 0.0, 0, 0).then_inc(S.g_deal, 1)
+
+    V.memset(T.onesf[:, :], 1.0).then_inc(S.ones, 1)
+    V.memset(T.onesb[:, :], 1.0).then_inc(S.ones, 1)
+    V.memset(T.inv[:, 0:2048], 0.0).then_inc(S.z1, 1)
+    V.memset(T.inv[:, 2048:ZS], 0.0).then_inc(S.z2, 1)
+    V.wait_ge(S.d_snd, 16)
+    V.tensor_copy(T.sfl[0:16, :], T.sraw[0:16, :]).then_inc(S.v_sf, 1)
+    V.wait_ge(S.p_e, 1)
+    V.tensor_copy(T.ecol[:, :], T.psE[:, 0:16]).then_inc(S.v_e, 1)
+    V.wait_ge(S.d_plc, 16)
+    V.tensor_copy(T.poff[:, :], T.praw[:, :]).then_inc(S.v_po, 1)
+    V.wait_ge(S.p_s, 1)
+    V.tensor_copy(T.soff[:, :], T.psS[:, 0:256]).then_inc(S.v_so, 1)
+    V.wait_ge(S.g_tl, 2)
+    V.wait_ge(S.v_e, 1)
+    V.tensor_scalar(T.vl[:, :], T.tl[:, :], T.ecol[:, 1:2], 0.125, AluOpType.mult, AluOpType.mult).then_inc(S.v_vl, 1)
+    V.wait_ge(S.v_vl, 1)
+    V.wait_ge(S.s_vh, 1)
+    V.tensor_tensor(T.vals[:, :], T.vl[:, :], T.vh[:, :], AluOpType.add).then_inc(S.v_val, 1)
+    V.wait_ge(S.v_val, 1)
+    V.wait_ge(S.v_po, 1)
+    V.wait_ge(S.z1, 1)
+    V.wait_ge(S.z2, 1)
+    V.wait_ge(S.z3, 1)
+    V.tensor_copy(T.inv[:, :].indirect(T.poff[:, 0:32]), T.vals[:, :]).then_inc(S.v_sc, 1)
+
+    A.wait_ge(S.z1, 1)
+    A.activation(T.inv[:, ZS:G], T.inv[:, 0:G - ZS], COPY).then_inc(S.z3, 1)
+    A.wait_ge(S.v_e, 1)
+    A.wait_ge(S.g_th, 1)
+    A.activation(T.vh[:, :], T.th[:, :], COPY, scale=T.ecol[:, 0:1]).then_inc(S.s_vh, 1)
+    A.wait_ge(S.p_c, 1)
+    A.activation(T.cown[:, :], T.psC[:, :], COPY).then_inc(S.s_c, 1)
+
+    P.wait_ge(S.g_rep, 1)
+    P.matmul(T.psE[:, 0:16], T.rep[0:16, :], T.rep[0:16, 0:16], True, True).then_inc(S.p_e, 1)
+    P.wait_ge(S.v_sf, 1)
+    P.matmul(T.psS[:, 0:256], T.rep[0:16, :], T.sfl[0:16, :], True, True).then_inc(S.p_s, 1)
+    P.wait_ge(S.g_c, 1)
+    P.matmul(T.psC[:, :], T.rep[0:16, :], T.crow[0:16, :], True, True).then_inc(S.p_c, 1)
+    P.wait_ge(S.g_deal, 1)
+    P.wait_ge(S.v_sc, 1)
+    for q in range(16):
+        m = P.matmul(T.psI[:, :], T.deal[:, 16 - q:144 - q], T.inv[:, q::16], q == 0, q == 15)
+        if q == 15:
+            m.then_inc(S.p_i, 1)
+
+    for eng in (V, A):
+        eng.wait_ge(S.d_x, 16)
+        eng.wait_ge(S.v_so, 1)
+    for i, (a, b) in enumerate(SEND):
+        V.tensor_copy(T.tolo[:, a:b], T.xs[:, :].indirect(T.soff[:, a // 16:b // 16])).then_inc(S["lo%d" % i], 1)
+        A.activation(T.tohi[:, a:b], T.xs[:, :].indirect(T.soff[:, (CAP + a) // 16:(CAP + b) // 16]), COPY,
+                     bias=-0.0).then_inc(S["hi%d" % i], 1)
+
+    for i, (a, b) in enumerate(SEND):
+        g.wait_ge(S["lo%d" % i], 1)
+        g.wait_ge(S["hi%d" % i], 1)
+        g.remote_dma_fused([
+            RemoteDMATransfer(dst_ids=[dest(topo, lo)], dma_engine_mask=mlo, remote_sem=S.fromhi,
+                              src=T.tolo[:, a:b], dst=T.win[:, G + CAP + a:G + CAP + b]),
+            RemoteDMATransfer(dst_ids=[dest(topo, hi)], dma_engine_mask=mhi, remote_sem=S.fromlo,
+                              src=T.tohi[:, a:b], dst=T.win[:, G + a:G + b]),
+        ], local_sem=S.left)
+    g.sem_inc(S.sent, 1)
+
+    Q.wait_ge(S.d_x, 16)
+    for i, (a, b) in enumerate(GH):
+        if i:
+            Q.wait_ge(S.sent, 1)
+        Q.dma_start(T.win[:, a:b], T.gh[:, a:b]).then_inc(S["d_gh%d" % i], 16)
+
+    V.wait_ge(S.p_i, 1)
+    V.wait_ge(S.s_c, 1)
+    V.tensor_tensor(T.mx[:, :], T.psI[:, :], T.cown[:, :], AluOpType.max).then_inc(S.v_mx, 1)
+    V.wait_ge(S.v_mx, 1)
+    V.tensor_copy(T.yoff[:, :], T.mx[:, :]).then_inc(S.v_off, 1)
+
+    for eng in (V, A):
+        eng.wait_ge(S.v_off, 1)
+        for i in range(len(GH)):
+            eng.wait_ge(S["d_gh%d" % i], 16)
+        eng.wait_ge(S.fromlo, len(SEND) * nhi)
+        eng.wait_ge(S.fromhi, len(SEND) * nlo)
+    for i, (a, b) in enumerate(VOUT):
+        V.tensor_copy(T.yt[:, a:b], T.win[:, :].indirect(T.yoff[:, a // 16:b // 16])).then_inc(S["yv%d" % i], 1)
+    for i, (a, b) in enumerate(SOUT):
+        A.activation(T.yt[:, a:b], T.win[:, :].indirect(T.yoff[:, a // 16:b // 16]), COPY, bias=-0.0).then_inc(S["ys%d" % i], 1)
+    for i in range(len(VOUT)):
+        for nm, (a, b) in (("yv%d" % i, VOUT[i]), ("ys%d" % i, SOUT[i])):
+            Q.wait_ge(S[nm], 1)
+            Q.dma_start(T.y[:, a:b], T.yt[:, a:b]).then_inc(S.d_y, 16)
+    Q.wait_ge(S.d_y, 16 * (len(VOUT) + len(SOUT)))
+    g.wait_ge(S.left, len(SEND) * (nlo + nhi))

@@ -7,9 +7,11 @@ WIN = G + 2 * CAP
 COPY = ActivationFunctionType.Copy
 
 SEND = [(0, 768), (768, 2048)]
-VOUT = [(0, 1024), (1024, 3072), (3072, 4096)]
-SOUT = [(4096, 5120), (5120, 7168), (7168, 8192)]
-GH = [(0, 2048), (2048, 8192)]
+VOUT = [(a, a + 1024) for a in range(0, 4096, 1024)]
+SOUT = [(a, a + 1024) for a in range(4096, 8192, 1024)]
+GH = [(0, 4096), (4096, 8192)]
+HELP = 2
+KH = G // 16 // HELP
 ZS = 6144
 
 SCRATCH = {
@@ -23,21 +25,23 @@ SCRATCH = {
     "sfl": ("sbuf", [128, 256], "float32"),
     "soff": ("sbuf", [128, 256], "uint16"),
     "praw": ("sbuf", [128, 32], "int32"),
+    "pin": ("sbuf", [128, 32], "int32"),
     "poff": ("sbuf", [128, 32], "uint16"),
     "onesf": ("sbuf", [128, 128], "float32"),
     "onesb": ("sbuf", [128, 144], "bfloat16"),
     "rep": ("sbuf", [128, 128], "float32"),
     "deal": ("sbuf", [128, 144], "bfloat16"),
-    "crow": ("sbuf", [128, 512], "float32"),
-    "cown": ("sbuf", [128, 512], "float32"),
+    "crow": ("sbuf", [128, KH], "float32"),
+    "cown": ("sbuf", [128, KH], "float32"),
     "tl": ("sbuf", [128, 512], "float32"),
     "th": ("sbuf", [128, 512], "float32"),
     "vl": ("sbuf", [128, 512], "bfloat16"),
     "vh": ("sbuf", [128, 512], "bfloat16"),
     "vals": ("sbuf", [128, 512], "bfloat16"),
     "ecol": ("sbuf", [128, 16], "float32"),
-    "mx": ("sbuf", [128, 512], "float32"),
-    "yoff": ("sbuf", [128, 512], "uint16"),
+    "mx": ("sbuf", [128, KH], "float32"),
+    "hoff": ("sbuf", [128, KH], "uint16"),
+    "yoff": ("sbuf", [128, G // 16], "uint16"),
     "psE": ("psum", [128, 512], "float32"),
     "psS": ("psum", [128, 512], "float32"),
     "psC": ("psum", [128, 512], "float32"),
@@ -45,7 +49,8 @@ SCRATCH = {
 }
 SEMAPHORES = (["d_snd", "d_plc", "d_x", "d_y", "ones", "z1", "z2", "z3", "g_rep", "g_c", "g_tl", "g_th", "g_deal",
                "v_sf", "v_po", "v_e", "v_vl", "v_so", "v_val", "v_sc", "v_mx", "v_off", "s_c", "s_vh",
-               "p_e", "p_s", "p_c", "p_i", "sent", "left", "fromlo", "fromhi"]
+               "p_e", "p_s", "p_c", "p_i", "sent", "left", "gotplc", "fromlo", "fromhi"]
+              + ["list%d" % i for i in range(HELP)]
               + ["d_gh%d" % i for i in range(len(GH))]
               + ["lo%d" % i for i in range(len(SEND))] + ["hi%d" % i for i in range(len(SEND))]
               + ["yv%d" % i for i in range(len(VOUT))] + ["ys%d" % i for i in range(len(SOUT))])
@@ -66,53 +71,50 @@ def dest(topo, c):
     return DstId(rid=rid, pnc=pid)
 
 
-def rank_program(g, core, T, topo):
-    rank = T.rank_of(core)
-    if rank is None:
-        return
-    S = T.sem
-    V, A, P, Q = g.vector, g.scalar, g.tensor, g.sync
-    lo, hi = T.cores[(rank - 1) % N], T.cores[(rank + 1) % N]
-    mlo, _ = halves(topo.mask(core, lo))
-    _, mhi = halves(topo.mask(core, hi))
-    nlo, nhi = len(bits(mlo)), len(bits(mhi))
+def helpers(T, topo, c):
+    return [h for h in range(128) if topo.chip(h) == topo.chip(c) and topo.die(h) == topo.die(c)
+            and T.rank_of(h) is None][:HELP]
 
-    Q.dma_start(T.sraw[0:16, :], T.snd[:, :]).then_inc(S.d_snd, 16)
-    Q.dma_start(T.xs[:, :], T.x[:, :]).then_inc(S.d_x, 16)
-    A.dma_start(T.praw[:, :], T.plc[:, :]).then_inc(S.d_plc, 16)
+
+def helper_program(g, core, owner, part, T, topo):
+    S = T.sem
+    V, A, P = g.vector, g.scalar, g.tensor
+    k0 = part * KH
+    back, _ = halves(topo.mask(core, owner))
 
     g.wait_ge(S.ones, 2)
     g.affine_select(T.rep[0:16, :], T.onesf[0:16, :], [[0, 8], [1, 16]], AluOpType.is_equal, 0.0, 0, -1).then_inc(S.g_rep, 1)
-    g.iota(T.crow[0:16, :], [[16, 512]], 0, 1, allow_small_or_imprecise_dtypes=True).then_inc(S.g_c, 1)
     g.iota(T.th[:, :], [[256, 2], [0, 32], [512, 8]], G, 0, allow_small_or_imprecise_dtypes=True).then_inc(S.g_th, 1)
     for a in (0, 256):
         g.iota(T.tl[:, a:a + 256], [[128, 16], [8, 2], [0, 8]], -1, 1, allow_small_or_imprecise_dtypes=True).then_inc(S.g_tl, 1)
+    g.iota(T.crow[0:16, :], [[16, KH]], 16 * k0, 1, allow_small_or_imprecise_dtypes=True).then_inc(S.g_c, 1)
     g.affine_select(T.deal[:, :], T.onesb[:, :], [[0, 9], [1, 16]], AluOpType.is_equal, 0.0, 0, 0).then_inc(S.g_deal, 1)
 
     V.memset(T.onesf[:, :], 1.0).then_inc(S.ones, 1)
     V.memset(T.onesb[:, :], 1.0).then_inc(S.ones, 1)
     V.memset(T.inv[:, 0:2048], 0.0).then_inc(S.z1, 1)
     V.memset(T.inv[:, 2048:ZS], 0.0).then_inc(S.z2, 1)
-    V.wait_ge(S.d_snd, 16)
-    V.tensor_copy(T.sfl[0:16, :], T.sraw[0:16, :]).then_inc(S.v_sf, 1)
     V.wait_ge(S.p_e, 1)
     V.tensor_copy(T.ecol[:, :], T.psE[:, 0:16]).then_inc(S.v_e, 1)
-    V.wait_ge(S.d_plc, 16)
-    V.tensor_copy(T.poff[:, :], T.praw[:, :]).then_inc(S.v_po, 1)
-    V.wait_ge(S.p_s, 1)
-    V.tensor_copy(T.soff[:, :], T.psS[:, 0:256]).then_inc(S.v_so, 1)
     V.wait_ge(S.g_tl, 2)
     V.wait_ge(S.v_e, 1)
     V.tensor_scalar(T.vl[:, :], T.tl[:, :], T.ecol[:, 1:2], 0.125, AluOpType.mult, AluOpType.mult).then_inc(S.v_vl, 1)
     V.wait_ge(S.v_vl, 1)
     V.wait_ge(S.s_vh, 1)
     V.tensor_tensor(T.vals[:, :], T.vl[:, :], T.vh[:, :], AluOpType.add).then_inc(S.v_val, 1)
+    V.wait_ge(S.gotplc, len(bits(topo.mask(owner, core))))
+    V.tensor_copy(T.poff[:, :], T.pin[:, :]).then_inc(S.v_po, 1)
     V.wait_ge(S.v_val, 1)
     V.wait_ge(S.v_po, 1)
     V.wait_ge(S.z1, 1)
     V.wait_ge(S.z2, 1)
     V.wait_ge(S.z3, 1)
     V.tensor_copy(T.inv[:, :].indirect(T.poff[:, 0:32]), T.vals[:, :]).then_inc(S.v_sc, 1)
+    V.wait_ge(S.p_i, 1)
+    V.wait_ge(S.s_c, 1)
+    V.tensor_tensor(T.mx[:, :], T.psI[:, 0:KH], T.cown[:, :], AluOpType.max).then_inc(S.v_mx, 1)
+    V.wait_ge(S.v_mx, 1)
+    V.tensor_copy(T.hoff[:, :], T.mx[:, :]).then_inc(S.v_off, 1)
 
     A.wait_ge(S.z1, 1)
     A.activation(T.inv[:, ZS:G], T.inv[:, 0:G - ZS], COPY).then_inc(S.z3, 1)
@@ -120,20 +122,61 @@ def rank_program(g, core, T, topo):
     A.wait_ge(S.g_th, 1)
     A.activation(T.vh[:, :], T.th[:, :], COPY, scale=T.ecol[:, 0:1]).then_inc(S.s_vh, 1)
     A.wait_ge(S.p_c, 1)
-    A.activation(T.cown[:, :], T.psC[:, :], COPY).then_inc(S.s_c, 1)
+    A.activation(T.cown[:, :], T.psC[:, 0:KH], COPY).then_inc(S.s_c, 1)
 
     P.wait_ge(S.g_rep, 1)
     P.matmul(T.psE[:, 0:16], T.rep[0:16, :], T.rep[0:16, 0:16], True, True).then_inc(S.p_e, 1)
-    P.wait_ge(S.v_sf, 1)
-    P.matmul(T.psS[:, 0:256], T.rep[0:16, :], T.sfl[0:16, :], True, True).then_inc(S.p_s, 1)
     P.wait_ge(S.g_c, 1)
-    P.matmul(T.psC[:, :], T.rep[0:16, :], T.crow[0:16, :], True, True).then_inc(S.p_c, 1)
+    P.matmul(T.psC[:, 0:KH], T.rep[0:16, :], T.crow[0:16, :], True, True).then_inc(S.p_c, 1)
     P.wait_ge(S.g_deal, 1)
     P.wait_ge(S.v_sc, 1)
     for q in range(16):
-        m = P.matmul(T.psI[:, :], T.deal[:, 16 - q:144 - q], T.inv[:, q::16], q == 0, q == 15)
+        m = P.matmul(T.psI[:, 0:KH], T.deal[:, 16 - q:144 - q], T.inv[:, 16 * k0 + q:16 * (k0 + KH):16], q == 0, q == 15)
         if q == 15:
             m.then_inc(S.p_i, 1)
+
+    rid, pid, _ = topo.addr(owner)
+    g.wait_ge(S.v_off, 1)
+    g.remote_dma(T.yoff[:, k0:k0 + KH], T.hoff[:, :], S["list%d" % part], S.left, pid, rid, back)
+    g.wait_ge(S.left, len(bits(back)))
+
+
+def rank_program(g, core, T, topo):
+    rank = T.rank_of(core)
+    if rank is None:
+        for c in T.cores:
+            hs = helpers(T, topo, c)
+            if core in hs:
+                helper_program(g, core, c, hs.index(core), T, topo)
+        return
+    S = T.sem
+    V, A, P, Q = g.vector, g.scalar, g.tensor, g.sync
+    lo, hi = T.cores[(rank - 1) % N], T.cores[(rank + 1) % N]
+    mlo, _ = halves(topo.mask(core, lo))
+    _, mhi = halves(topo.mask(core, hi))
+    nlo, nhi = len(bits(mlo)), len(bits(mhi))
+    hs = helpers(T, topo, core)
+
+    Q.dma_start(T.sraw[0:16, :], T.snd[:, :]).then_inc(S.d_snd, 16)
+    A.dma_start(T.praw[:, :], T.plc[:, :]).then_inc(S.d_plc, 16)
+    Q.dma_start(T.xs[:, :], T.x[:, :]).then_inc(S.d_x, 16)
+
+    V.memset(T.onesf[:, :], 1.0).then_inc(S.ones, 1)
+    g.wait_ge(S.ones, 1)
+    g.affine_select(T.rep[0:16, :], T.onesf[0:16, :], [[0, 8], [1, 16]], AluOpType.is_equal, 0.0, 0, -1).then_inc(S.g_rep, 1)
+    V.wait_ge(S.d_snd, 16)
+    V.tensor_copy(T.sfl[0:16, :], T.sraw[0:16, :]).then_inc(S.v_sf, 1)
+    P.wait_ge(S.g_rep, 1)
+    P.wait_ge(S.v_sf, 1)
+    P.matmul(T.psS[:, 0:256], T.rep[0:16, :], T.sfl[0:16, :], True, True).then_inc(S.p_s, 1)
+    V.wait_ge(S.p_s, 1)
+    V.tensor_copy(T.soff[:, :], T.psS[:, 0:256]).then_inc(S.v_so, 1)
+
+    g.wait_ge(S.d_plc, 16)
+    g.remote_dma_fused([
+        RemoteDMATransfer(dst_ids=[dest(topo, h) for h in hs], dma_engine_mask=topo.mask(core, hs[0]), remote_sem=S.gotplc,
+                          srcs=[T.praw[:, :]], dsts=[T.pin[:, :] for h in hs]),
+    ], local_sem=S.left)
 
     for eng in (V, A):
         eng.wait_ge(S.d_x, 16)
@@ -154,22 +197,16 @@ def rank_program(g, core, T, topo):
         ], local_sem=S.left)
     g.sem_inc(S.sent, 1)
 
-    Q.wait_ge(S.d_x, 16)
     for i, (a, b) in enumerate(GH):
         if i:
             Q.wait_ge(S.sent, 1)
         Q.dma_start(T.win[:, a:b], T.gh[:, a:b]).then_inc(S["d_gh%d" % i], 16)
 
-    V.wait_ge(S.p_i, 1)
-    V.wait_ge(S.s_c, 1)
-    V.tensor_tensor(T.mx[:, :], T.psI[:, :], T.cown[:, :], AluOpType.max).then_inc(S.v_mx, 1)
-    V.wait_ge(S.v_mx, 1)
-    V.tensor_copy(T.yoff[:, :], T.mx[:, :]).then_inc(S.v_off, 1)
-
     for eng in (V, A):
-        eng.wait_ge(S.v_off, 1)
         for i in range(len(GH)):
             eng.wait_ge(S["d_gh%d" % i], 16)
+        for i, h in enumerate(hs):
+            eng.wait_ge(S["list%d" % i], len(bits(halves(topo.mask(h, core))[0])))
         eng.wait_ge(S.fromlo, len(SEND) * nhi)
         eng.wait_ge(S.fromhi, len(SEND) * nlo)
     for i, (a, b) in enumerate(VOUT):
@@ -181,4 +218,4 @@ def rank_program(g, core, T, topo):
             Q.wait_ge(S[nm], 1)
             Q.dma_start(T.y[:, a:b], T.yt[:, a:b]).then_inc(S.d_y, 16)
     Q.wait_ge(S.d_y, 16 * (len(VOUT) + len(SOUT)))
-    g.wait_ge(S.left, len(SEND) * (nlo + nhi))
+    g.wait_ge(S.left, len(SEND) * (nlo + nhi) + len(bits(topo.mask(core, hs[0]))))

from concourse.bass import DstId, RemoteDMATransfer
from concourse.mybir import AluOpType, ActivationFunctionType

N = 16
TX, G, CAP = 8192, 8192, 2048
WIN = G + 2 * CAP
COPY = ActivationFunctionType.Copy

SEND = [(0, 768), (768, 2048)]
VOUT = [(a, a + 1024) for a in range(0, 4096, 1024)]
SOUT = [(a, a + 1024) for a in range(4096, 8192, 1024)]
GH = [(0, 4096), (4096, 8192)]
HELP = 2
KH = G // 16 // HELP
ZS = 6144

SCRATCH = {
    "xs": ("sbuf", [128, TX], "bfloat16"),
    "win": ("sbuf", [128, WIN], "bfloat16"),
    "yt": ("sbuf", [128, G], "bfloat16"),
    "tolo": ("sbuf", [128, CAP], "bfloat16"),
    "tohi": ("sbuf", [128, CAP], "bfloat16"),
    "inv": ("sbuf", [128, G], "bfloat16"),
    "sraw": ("sbuf", [128, 256], "int32"),
    "sfl": ("sbuf", [128, 256], "float32"),
    "soff": ("sbuf", [128, 256], "uint16"),
    "praw": ("sbuf", [128, 32], "int32"),
    "pin": ("sbuf", [128, 32], "int32"),
    "poff": ("sbuf", [128, 32], "uint16"),
    "onesf": ("sbuf", [128, 128], "float32"),
    "onesb": ("sbuf", [128, 144], "bfloat16"),
    "rep": ("sbuf", [128, 128], "float32"),
    "deal": ("sbuf", [128, 144], "bfloat16"),
    "crow": ("sbuf", [128, KH], "float32"),
    "cown": ("sbuf", [128, KH], "float32"),
    "tl": ("sbuf", [128, 512], "float32"),
    "th": ("sbuf", [128, 512], "float32"),
    "vl": ("sbuf", [128, 512], "bfloat16"),
    "vh": ("sbuf", [128, 512], "bfloat16"),
    "vals": ("sbuf", [128, 512], "bfloat16"),
    "ecol": ("sbuf", [128, 16], "float32"),
    "mx": ("sbuf", [128, KH], "float32"),
    "hoff": ("sbuf", [128, KH], "uint16"),
    "yoff": ("sbuf", [128, G // 16], "uint16"),
    "psE": ("psum", [128, 512], "float32"),
    "psS": ("psum", [128, 512], "float32"),
    "psC": ("psum", [128, 512], "float32"),
    "psI": ("psum", [128, 512], "float32"),
}
SEMAPHORES = (["d_snd", "d_plc", "d_x", "d_y", "ones", "z1", "z2", "z3", "g_rep", "g_c", "g_tl", "g_th", "g_deal",
               "v_sf", "v_po", "v_e", "v_vl", "v_so", "v_val", "v_sc", "v_mx", "v_off", "s_c", "s_vh",
               "p_e", "p_s", "p_c", "p_i", "sent", "left", "gotplc", "fromlo", "fromhi"]
              + ["list%d" % i for i in range(HELP)]
              + ["d_gh%d" % i for i in range(len(GH))]
              + ["lo%d" % i for i in range(len(SEND))] + ["hi%d" % i for i in range(len(SEND))]
              + ["yv%d" % i for i in range(len(VOUT))] + ["ys%d" % i for i in range(len(SOUT))])


def bits(mask):
    return [b for b in range(mask.bit_length()) if mask >> b & 1]


def halves(mask):
    b = bits(mask)
    h = len(b) // 2
    return sum(1 << i for i in b[:h]), sum(1 << i for i in b[h:])


def dest(topo, c):
    rid, pid, _ = topo.addr(c)
    return DstId(rid=rid, pnc=pid)


def helpers(T, topo, c):
    return [h for h in range(128) if topo.chip(h) == topo.chip(c) and topo.die(h) == topo.die(c)
            and T.rank_of(h) is None][:HELP]


def helper_program(g, core, owner, part, T, topo):
    S = T.sem
    V, A, P = g.vector, g.scalar, g.tensor
    k0 = part * KH
    back, _ = halves(topo.mask(core, owner))

    g.wait_ge(S.ones, 2)
    g.affine_select(T.rep[0:16, :], T.onesf[0:16, :], [[0, 8], [1, 16]], AluOpType.is_equal, 0.0, 0, -1).then_inc(S.g_rep, 1)
    g.iota(T.th[:, :], [[256, 2], [0, 32], [512, 8]], G, 0, allow_small_or_imprecise_dtypes=True).then_inc(S.g_th, 1)
    for a in (0, 256):
        g.iota(T.tl[:, a:a + 256], [[128, 16], [8, 2], [0, 8]], -1, 1, allow_small_or_imprecise_dtypes=True).then_inc(S.g_tl, 1)
    g.iota(T.crow[0:16, :], [[16, KH]], 16 * k0, 1, allow_small_or_imprecise_dtypes=True).then_inc(S.g_c, 1)
    g.affine_select(T.deal[:, :], T.onesb[:, :], [[0, 9], [1, 16]], AluOpType.is_equal, 0.0, 0, 0).then_inc(S.g_deal, 1)

    V.memset(T.onesf[:, :], 1.0).then_inc(S.ones, 1)
    V.memset(T.onesb[:, :], 1.0).then_inc(S.ones, 1)
    V.memset(T.inv[:, 0:2048], 0.0).then_inc(S.z1, 1)
    V.memset(T.inv[:, 2048:ZS], 0.0).then_inc(S.z2, 1)
    V.wait_ge(S.p_e, 1)
    V.tensor_copy(T.ecol[:, :], T.psE[:, 0:16]).then_inc(S.v_e, 1)
    V.wait_ge(S.g_tl, 2)
    V.wait_ge(S.v_e, 1)
    V.tensor_scalar(T.vl[:, :], T.tl[:, :], T.ecol[:, 1:2], 0.125, AluOpType.mult, AluOpType.mult).then_inc(S.v_vl, 1)
    V.wait_ge(S.v_vl, 1)
    V.wait_ge(S.s_vh, 1)
    V.tensor_tensor(T.vals[:, :], T.vl[:, :], T.vh[:, :], AluOpType.add).then_inc(S.v_val, 1)
    V.wait_ge(S.gotplc, len(bits(topo.mask(owner, core))))
    V.tensor_copy(T.poff[:, :], T.pin[:, :]).then_inc(S.v_po, 1)
    V.wait_ge(S.v_val, 1)
    V.wait_ge(S.v_po, 1)
    V.wait_ge(S.z1, 1)
    V.wait_ge(S.z2, 1)
    V.wait_ge(S.z3, 1)
    V.tensor_copy(T.inv[:, :].indirect(T.poff[:, 0:32]), T.vals[:, :]).then_inc(S.v_sc, 1)
    V.wait_ge(S.p_i, 1)
    V.wait_ge(S.s_c, 1)
    V.tensor_tensor(T.mx[:, :], T.psI[:, 0:KH], T.cown[:, :], AluOpType.max).then_inc(S.v_mx, 1)
    V.wait_ge(S.v_mx, 1)
    V.tensor_copy(T.hoff[:, :], T.mx[:, :]).then_inc(S.v_off, 1)

    A.wait_ge(S.z1, 1)
    A.activation(T.inv[:, ZS:G], T.inv[:, 0:G - ZS], COPY).then_inc(S.z3, 1)
    A.wait_ge(S.v_e, 1)
    A.wait_ge(S.g_th, 1)
    A.activation(T.vh[:, :], T.th[:, :], COPY, scale=T.ecol[:, 0:1]).then_inc(S.s_vh, 1)
    A.wait_ge(S.p_c, 1)
    A.activation(T.cown[:, :], T.psC[:, 0:KH], COPY).then_inc(S.s_c, 1)

    P.wait_ge(S.g_rep, 1)
    P.matmul(T.psE[:, 0:16], T.rep[0:16, :], T.rep[0:16, 0:16], True, True).then_inc(S.p_e, 1)
    P.wait_ge(S.g_c, 1)
    P.matmul(T.psC[:, 0:KH], T.rep[0:16, :], T.crow[0:16, :], True, True).then_inc(S.p_c, 1)
    P.wait_ge(S.g_deal, 1)
    P.wait_ge(S.v_sc, 1)
    for q in range(16):
        m = P.matmul(T.psI[:, 0:KH], T.deal[:, 16 - q:144 - q], T.inv[:, 16 * k0 + q:16 * (k0 + KH):16], q == 0, q == 15)
        if q == 15:
            m.then_inc(S.p_i, 1)

    rid, pid, _ = topo.addr(owner)
    g.wait_ge(S.v_off, 1)
    g.remote_dma(T.yoff[:, k0:k0 + KH], T.hoff[:, :], S["list%d" % part], S.left, pid, rid, back)
    g.wait_ge(S.left, len(bits(back)))


def rank_program(g, core, T, topo):
    rank = T.rank_of(core)
    if rank is None:
        for c in T.cores:
            hs = helpers(T, topo, c)
            if core in hs:
                helper_program(g, core, c, hs.index(core), T, topo)
        return
    S = T.sem
    V, A, P, Q = g.vector, g.scalar, g.tensor, g.sync
    lo, hi = T.cores[(rank - 1) % N], T.cores[(rank + 1) % N]
    mlo, _ = halves(topo.mask(core, lo))
    _, mhi = halves(topo.mask(core, hi))
    nlo, nhi = len(bits(mlo)), len(bits(mhi))
    hs = helpers(T, topo, core)

    Q.dma_start(T.sraw[0:16, :], T.snd[:, :]).then_inc(S.d_snd, 16)
    A.dma_start(T.praw[:, :], T.plc[:, :]).then_inc(S.d_plc, 16)
    Q.dma_start(T.xs[:, :], T.x[:, :]).then_inc(S.d_x, 16)

    V.memset(T.onesf[:, :], 1.0).then_inc(S.ones, 1)
    g.wait_ge(S.ones, 1)
    g.affine_select(T.rep[0:16, :], T.onesf[0:16, :], [[0, 8], [1, 16]], AluOpType.is_equal, 0.0, 0, -1).then_inc(S.g_rep, 1)
    V.wait_ge(S.d_snd, 16)
    V.tensor_copy(T.sfl[0:16, :], T.sraw[0:16, :]).then_inc(S.v_sf, 1)
    P.wait_ge(S.g_rep, 1)
    P.wait_ge(S.v_sf, 1)
    P.matmul(T.psS[:, 0:256], T.rep[0:16, :], T.sfl[0:16, :], True, True).then_inc(S.p_s, 1)
    V.wait_ge(S.p_s, 1)
    V.tensor_copy(T.soff[:, :], T.psS[:, 0:256]).then_inc(S.v_so, 1)

    g.wait_ge(S.d_plc, 16)
    g.remote_dma_fused([
        RemoteDMATransfer(dst_ids=[dest(topo, h) for h in hs], dma_engine_mask=topo.mask(core, hs[0]), remote_sem=S.gotplc,
                          srcs=[T.praw[:, :]], dsts=[T.pin[:, :] for h in hs]),
    ], local_sem=S.left)

    for eng in (V, A):
        eng.wait_ge(S.d_x, 16)
        eng.wait_ge(S.v_so, 1)
    for i, (a, b) in enumerate(SEND):
        V.tensor_copy(T.tolo[:, a:b], T.xs[:, :].indirect(T.soff[:, a // 16:b // 16])).then_inc(S["lo%d" % i], 1)
        A.activation(T.tohi[:, a:b], T.xs[:, :].indirect(T.soff[:, (CAP + a) // 16:(CAP + b) // 16]), COPY,
                     bias=-0.0).then_inc(S["hi%d" % i], 1)

    for i, (a, b) in enumerate(SEND):
        g.wait_ge(S["lo%d" % i], 1)
        g.wait_ge(S["hi%d" % i], 1)
        g.remote_dma_fused([
            RemoteDMATransfer(dst_ids=[dest(topo, lo)], dma_engine_mask=mlo, remote_sem=S.fromhi,
                              src=T.tolo[:, a:b], dst=T.win[:, G + CAP + a:G + CAP + b]),
            RemoteDMATransfer(dst_ids=[dest(topo, hi)], dma_engine_mask=mhi, remote_sem=S.fromlo,
                              src=T.tohi[:, a:b], dst=T.win[:, G + a:G + b]),
        ], local_sem=S.left)
    g.sem_inc(S.sent, 1)

    for i, (a, b) in enumerate(GH):
        if i:
            Q.wait_ge(S.sent, 1)
        Q.dma_start(T.win[:, a:b], T.gh[:, a:b]).then_inc(S["d_gh%d" % i], 16)

    for eng in (V, A):
        for i in range(len(GH)):
            eng.wait_ge(S["d_gh%d" % i], 16)
        for i, h in enumerate(hs):
            eng.wait_ge(S["list%d" % i], len(bits(halves(topo.mask(h, core))[0])))
        eng.wait_ge(S.fromlo, len(SEND) * nhi)
        eng.wait_ge(S.fromhi, len(SEND) * nlo)
    for i, (a, b) in enumerate(VOUT):
        V.tensor_copy(T.yt[:, a:b], T.win[:, :].indirect(T.yoff[:, a // 16:b // 16])).then_inc(S["yv%d" % i], 1)
    for i, (a, b) in enumerate(SOUT):
        A.activation(T.yt[:, a:b], T.win[:, :].indirect(T.yoff[:, a // 16:b // 16]), COPY, bias=-0.0).then_inc(S["ys%d" % i], 1)
    for i in range(len(VOUT)):
        for nm, (a, b) in (("yv%d" % i, VOUT[i]), ("ys%d" % i, SOUT[i])):
            Q.wait_ge(S[nm], 1)
            Q.dma_start(T.y[:, a:b], T.yt[:, a:b]).then_inc(S.d_y, 16)
    Q.wait_ge(S.d_y, 16 * (len(VOUT) + len(SOUT)))
    g.wait_ge(S.left, len(SEND) * (nlo + nhi) + len(bits(topo.mask(core, hs[0]))))
